import numpy as np
import ml_dtypes

BF16 = ml_dtypes.bfloat16


def bf(x):
    return np.asarray(x, np.float32).astype(BF16)


def f32(x):
    return np.asarray(x, np.float32)


def f64(x):
    return np.asarray(x).astype(np.float64)


def striped(idx):
    return np.tile(idx.reshape(-1, 16).T, (8, 1))


def rows(idx, k):
    return np.tile(idx, (k, 1))


def look(tab, idx):
    return np.take_along_axis(f64(tab), rows(idx, len(tab)), axis=1)


K, S, V, N = 128, 2048, 2048, 2048


def setup_inputs():
    return {"tab": f32(np.random.standard_normal((2, K, S))), "y": f32(np.random.standard_normal((K, V))), "offs": striped(np.random.permutation(S)[:N])}


def reference(tab, y, offs):
    idx = offs[:16].T.reshape(-1)
    x = (np.minimum(look(tab[0], idx), f64(y))) * (np.tanh(look(tab[1], idx)))
    return x

@@ -1,0 +1,37 @@
+import concourse.mybir as mybir
+
+F32 = mybir.dt.float32
+U16 = mybir.dt.uint16
+ENTRIES_PER_COLUMN = 16
+PIECE = 512
+
+
+def tile_lookup_vg_mintanh_out_kernel(tc, tab, y, offs, out):
+    nc = tc.nc
+    rows, places = tab.shape[1], tab.shape[2]
+    entries = y.shape[1]
+    pieces = entries // PIECE
+
+    with (
+        tc.tile_pool(name="held", bufs=1) as held,
+        tc.tile_pool(name="work", bufs=pieces) as work,
+    ):
+        offsets = held.tile([rows, entries // ENTRIES_PER_COLUMN], U16, name="offsets")
+        values = held.tile([rows, places], F32, name="values")
+        gates = held.tile([rows, places], F32, name="gates")
+        stream = held.tile([rows, entries], F32, name="stream")
+        nc.sync.dma_start(offsets[:], offs)
+        nc.sync.dma_start(values[:], tab[0])
+        nc.sync.dma_start(gates[:], tab[1])
+        nc.sync.dma_start(stream[:], y)
+
+        for start in range(0, entries, PIECE):
+            stop = start + PIECE
+            listed = offsets[:, start // ENTRIES_PER_COLUMN : stop // ENTRIES_PER_COLUMN]
+            clipped = work.tile([rows, PIECE], F32, name="clipped")
+            gate = work.tile([rows, PIECE], F32, name="gate")
+            product = work.tile([rows, PIECE], F32, name="product")
+            nc.vector.tensor_tensor(clipped[:], values[:].indirect(listed), stream[:, start:stop], mybir.AluOpType.min)
+            nc.scalar.activation(gate[:], gates[:].indirect(listed), mybir.ActivationFunctionType.Tanh)
+            nc.vector.tensor_tensor(product[:], clipped[:], gate[:], mybir.AluOpType.mult)
+            nc.sync.dma_start(out[:, start:stop], product[:])

@@ -10,28 +10,44 @@ def tile_lookup_vg_mintanh_out_kernel(tc, tab, y, offs, out):
     nc = tc.nc
     rows, places = tab.shape[1], tab.shape[2]
     entries = y.shape[1]
-    pieces = entries // PIECE
+    half = entries // 2
 
-    with (
-        tc.tile_pool(name="held", bufs=1) as held,
-        tc.tile_pool(name="work", bufs=pieces) as work,
-    ):
+    with tc.tile_pool(name="held", bufs=1) as held:
+        dummy = held.tile([rows, 1], F32, name="dummy")
+        dummy_tanh = held.tile([rows, 1], F32, name="dummy_tanh")
+        nc.vector.memset(dummy[:], 0.0)
+        nc.scalar.activation(dummy_tanh[:], dummy[:], mybir.ActivationFunctionType.Tanh)
+
         offsets = held.tile([rows, entries // ENTRIES_PER_COLUMN], U16, name="offsets")
         values = held.tile([rows, places], F32, name="values")
         gates = held.tile([rows, places], F32, name="gates")
         stream = held.tile([rows, entries], F32, name="stream")
-        nc.sync.dma_start(offsets[:], offs)
+        clipped = held.tile([rows, entries], F32, name="clipped")
+        opened = held.tile([rows, entries], F32, name="opened")
+        product = held.tile([rows, entries], F32, name="product")
+
+        def listed(start, stop):
+            return offsets[:, start // ENTRIES_PER_COLUMN : stop // ENTRIES_PER_COLUMN]
+
         nc.sync.dma_start(values[:], tab[0])
+        nc.sync.dma_start(offsets[:], offs)
+        nc.sync.dma_start(stream[:, :half], y[:, :half])
         nc.sync.dma_start(gates[:], tab[1])
-        nc.sync.dma_start(stream[:], y)
+        for start in range(half, entries, PIECE):
+            nc.sync.dma_start(stream[:, start : start + PIECE], y[:, start : start + PIECE])
 
         for start in range(0, entries, PIECE):
             stop = start + PIECE
-            listed = offsets[:, start // ENTRIES_PER_COLUMN : stop // ENTRIES_PER_COLUMN]
-            clipped = work.tile([rows, PIECE], F32, name="clipped")
-            gate = work.tile([rows, PIECE], F32, name="gate")
-            product = work.tile([rows, PIECE], F32, name="product")
-            nc.vector.tensor_tensor(clipped[:], values[:].indirect(listed), stream[:, start:stop], mybir.AluOpType.min)
-            nc.scalar.activation(gate[:], gates[:].indirect(listed), mybir.ActivationFunctionType.Tanh)
-            nc.vector.tensor_tensor(product[:], clipped[:], gate[:], mybir.AluOpType.mult)
-            nc.sync.dma_start(out[:, start:stop], product[:])
+            nc.vector.tensor_tensor(
+                clipped[:, start:stop], values[:].indirect(listed(start, stop)), stream[:, start:stop], mybir.AluOpType.min
+            )
+
+        cuts = list(range(0, entries, PIECE)) + [entries - PIECE // 2, entries]
+        for start, stop in zip(cuts, cuts[1:]):
+            nc.scalar.activation(
+                opened[:, start:stop], gates[:].indirect(listed(start, stop)), mybir.ActivationFunctionType.Tanh
+            )
+            nc.vector.tensor_tensor(
+                product[:, start:stop], clipped[:, start:stop], opened[:, start:stop], mybir.AluOpType.mult
+            )
+            nc.sync.dma_start(out[:, start:stop], product[:, start:stop])

@@ -42,7 +42,7 @@ def tile_lookup_vg_mintanh_out_kernel(tc, tab, y, offs, out):
                 clipped[:, start:stop], values[:].indirect(listed(start, stop)), stream[:, start:stop], mybir.AluOpType.min
             )
 
-        cuts = list(range(0, entries, PIECE)) + [entries - PIECE // 2, entries]
+        cuts = list(range(0, entries, PIECE)) + [entries - PIECE // 2, entries - PIECE // 4, entries]
         for start, stop in zip(cuts, cuts[1:]):
             nc.scalar.activation(
                 opened[:, start:stop], gates[:].indirect(listed(start, stop)), mybir.ActivationFunctionType.Tanh

@@ -29,9 +29,9 @@ def tile_lookup_vg_mintanh_out_kernel(tc, tab, y, offs, out):
         def listed(start, stop):
             return offsets[:, start // ENTRIES_PER_COLUMN : stop // ENTRIES_PER_COLUMN]
 
-        nc.sync.dma_start(values[:], tab[0])
         nc.sync.dma_start(offsets[:], offs)
-        nc.sync.dma_start(stream[:, :half], y[:, :half])
+        nc.sync.dma_start(values[:], tab[0])
+        nc.scalar.dma_start(stream[:, :half], y[:, :half])
         nc.sync.dma_start(gates[:], tab[1])
         for start in range(half, entries, PIECE):
             nc.sync.dma_start(stream[:, start : start + PIECE], y[:, start : start + PIECE])

@@ -29,25 +29,42 @@ def tile_lookup_vg_mintanh_out_kernel(tc, tab, y, offs, out):
         def listed(start, stop):
             return offsets[:, start // ENTRIES_PER_COLUMN : stop // ENTRIES_PER_COLUMN]
 
-        nc.sync.dma_start(offsets[:], offs)
-        nc.sync.dma_start(values[:], tab[0])
-        nc.scalar.dma_start(stream[:, :half], y[:, :half])
-        nc.sync.dma_start(gates[:], tab[1])
-        for start in range(half, entries, PIECE):
-            nc.sync.dma_start(stream[:, start : start + PIECE], y[:, start : start + PIECE])
-
-        for start in range(0, entries, PIECE):
-            stop = start + PIECE
+        def clip(start, stop):
             nc.vector.tensor_tensor(
                 clipped[:, start:stop], values[:].indirect(listed(start, stop)), stream[:, start:stop], mybir.AluOpType.min
             )
 
-        cuts = list(range(0, entries, PIECE)) + [entries - PIECE // 2, entries - PIECE // 4, entries]
-        for start, stop in zip(cuts, cuts[1:]):
+        def open_gates(start, stop):
             nc.scalar.activation(
                 opened[:, start:stop], gates[:].indirect(listed(start, stop)), mybir.ActivationFunctionType.Tanh
             )
+
+        def finish(start, stop):
             nc.vector.tensor_tensor(
                 product[:, start:stop], clipped[:, start:stop], opened[:, start:stop], mybir.AluOpType.mult
             )
             nc.sync.dma_start(out[:, start:stop], product[:, start:stop])
+
+        early = half - PIECE // 4
+        third = early + PIECE
+        nc.sync.dma_start(offsets[:], offs)
+        nc.sync.dma_start(values[:], tab[0])
+        nc.scalar.dma_start(stream[:, :early], y[:, :early])
+        nc.sync.dma_start(gates[:], tab[1])
+        nc.sync.dma_start(stream[:, early:third], y[:, early:third])
+        nc.sync.dma_start(stream[:, third:], y[:, third:])
+
+        cuts = list(range(0, entries, PIECE)) + [entries - PIECE // 2, entries - PIECE // 4, entries]
+        pieces = list(zip(cuts, cuts[1:]))
+        for start, stop in pieces:
+            open_gates(start, stop)
+
+        clip(0, early)
+        clip(early, third)
+        finish(*pieces[0])
+        clip(third, pieces[-1][0])
+        finish(*pieces[1])
+        finish(*pieces[2])
+        clip(*pieces[-1])
+        for start, stop in pieces[3:]:
+            finish(start, stop)

@@ -3,14 +3,14 @@ import concourse.mybir as mybir
 F32 = mybir.dt.float32
 U16 = mybir.dt.uint16
 ENTRIES_PER_COLUMN = 16
-PIECE = 512
+WIDE = 512
+NARROW = WIDE // 4
 
 
 def tile_lookup_vg_mintanh_out_kernel(tc, tab, y, offs, out):
     nc = tc.nc
     rows, places = tab.shape[1], tab.shape[2]
     entries = y.shape[1]
-    half = entries // 2
 
     with tc.tile_pool(name="held", bufs=1) as held:
         dummy = held.tile([rows, 1], F32, name="dummy")
@@ -45,26 +45,30 @@ def tile_lookup_vg_mintanh_out_kernel(tc, tab, y, offs, out):
             )
             nc.sync.dma_start(out[:, start:stop], product[:, start:stop])
 
-        early = half - PIECE // 4
-        third = early + PIECE
+        early = entries // 2 - NARROW
+        middle = early + WIDE
         nc.sync.dma_start(offsets[:], offs)
         nc.sync.dma_start(values[:], tab[0])
         nc.scalar.dma_start(stream[:, :early], y[:, :early])
         nc.sync.dma_start(gates[:], tab[1])
-        nc.sync.dma_start(stream[:, early:third], y[:, early:third])
-        nc.sync.dma_start(stream[:, third:], y[:, third:])
+        nc.sync.dma_start(stream[:, early:middle], y[:, early:middle])
+        nc.sync.dma_start(stream[:, middle:], y[:, middle:])
 
-        cuts = list(range(0, entries, PIECE)) + [entries - PIECE // 2, entries - PIECE // 4, entries]
+        last = entries - WIDE
+        for start in range(0, last, WIDE // 2):
+            open_gates(start, start + WIDE // 2)
+        for start in range(last, entries, NARROW):
+            open_gates(start, start + NARROW)
+
+        cuts = list(range(0, entries, WIDE)) + [entries - 2 * NARROW, entries - NARROW, entries]
         pieces = list(zip(cuts, cuts[1:]))
-        for start, stop in pieces:
-            open_gates(start, stop)
 
         clip(0, early)
-        clip(early, third)
+        clip(early, middle)
         finish(*pieces[0])
-        clip(third, pieces[-1][0])
+        clip(middle, entries - NARROW)
         finish(*pieces[1])
         finish(*pieces[2])
-        clip(*pieces[-1])
+        clip(entries - NARROW, entries)
         for start, stop in pieces[3:]:
             finish(start, stop)

@@ -24,7 +24,7 @@ def tile_lookup_vg_mintanh_out_kernel(tc, tab, y, offs, out):
         stream = held.tile([rows, entries], F32, name="stream")
         clipped = held.tile([rows, entries], F32, name="clipped")
         opened = held.tile([rows, entries], F32, name="opened")
-        product = held.tile([rows, entries], F32, name="product")
+        product = held.tile([rows, entries - 2 * WIDE], F32, name="product")
 
         def listed(start, stop):
             return offsets[:, start // ENTRIES_PER_COLUMN : stop // ENTRIES_PER_COLUMN]
@@ -39,20 +39,19 @@ def tile_lookup_vg_mintanh_out_kernel(tc, tab, y, offs, out):
                 opened[:, start:stop], gates[:].indirect(listed(start, stop)), mybir.ActivationFunctionType.Tanh
             )
 
-        def finish(start, stop):
-            nc.vector.tensor_tensor(
-                product[:, start:stop], clipped[:, start:stop], opened[:, start:stop], mybir.AluOpType.mult
-            )
-            nc.sync.dma_start(out[:, start:stop], product[:, start:stop])
+        def finish(start, stop, room):
+            nc.vector.tensor_tensor(room, clipped[:, start:stop], opened[:, start:stop], mybir.AluOpType.mult)
+            nc.sync.dma_start(out[:, start:stop], room)
 
         early = entries // 2 - NARROW
-        middle = early + WIDE
+        first = early + 2 * NARROW
+        second = first + 2 * NARROW
         nc.sync.dma_start(offsets[:], offs)
         nc.sync.dma_start(values[:], tab[0])
         nc.scalar.dma_start(stream[:, :early], y[:, :early])
         nc.sync.dma_start(gates[:], tab[1])
-        nc.sync.dma_start(stream[:, early:middle], y[:, early:middle])
-        nc.sync.dma_start(stream[:, middle:], y[:, middle:])
+        for start, stop in ((early, first), (first, second), (second, entries)):
+            nc.sync.dma_start(stream[:, start:stop], y[:, start:stop])
 
         last = entries - WIDE
         for start in range(0, last, WIDE // 2):
@@ -60,15 +59,17 @@ def tile_lookup_vg_mintanh_out_kernel(tc, tab, y, offs, out):
         for start in range(last, entries, NARROW):
             open_gates(start, start + NARROW)
 
-        cuts = list(range(0, entries, WIDE)) + [entries - 2 * NARROW, entries - NARROW, entries]
-        pieces = list(zip(cuts, cuts[1:]))
-
+        used = first + NARROW
         clip(0, early)
-        clip(early, middle)
-        finish(*pieces[0])
-        clip(middle, entries - NARROW)
-        finish(*pieces[1])
-        finish(*pieces[2])
+        clip(early, first)
+        clip(first, used)
+        clip(used, second)
+        finish(0, WIDE, stream[:, used - WIDE : used])
+        clip(second, used + WIDE)
+        clip(used + WIDE, entries - NARROW)
+        finish(WIDE, 2 * WIDE, stream[:, used : used + WIDE])
+        finish(2 * WIDE, last, product[:, :WIDE])
         clip(entries - NARROW, entries)
-        for start, stop in pieces[3:]:
-            finish(start, stop)
+        cuts = [last, entries - 2 * NARROW, entries - NARROW, entries]
+        for start, stop in zip(cuts, cuts[1:]):
+            finish(start, stop, product[:, start - 2 * WIDE : stop - 2 * WIDE])

@@ -4,7 +4,9 @@ F32 = mybir.dt.float32
 U16 = mybir.dt.uint16
 ENTRIES_PER_COLUMN = 16
 WIDE = 512
+HALF = WIDE // 2
 NARROW = WIDE // 4
+TINY = WIDE // 8
 
 
 def tile_lookup_vg_mintanh_out_kernel(tc, tab, y, offs, out):
@@ -24,14 +26,17 @@ def tile_lookup_vg_mintanh_out_kernel(tc, tab, y, offs, out):
         stream = held.tile([rows, entries], F32, name="stream")
         clipped = held.tile([rows, entries], F32, name="clipped")
         opened = held.tile([rows, entries], F32, name="opened")
-        product = held.tile([rows, entries - 2 * WIDE], F32, name="product")
 
         def listed(start, stop):
             return offsets[:, start // ENTRIES_PER_COLUMN : stop // ENTRIES_PER_COLUMN]
 
-        def clip(start, stop):
+        def streamed(start, stop):
+            place = (start + WIDE) % entries
+            return stream[:, place : place + stop - start]
+
+        def clip(start, stop, room):
             nc.vector.tensor_tensor(
-                clipped[:, start:stop], values[:].indirect(listed(start, stop)), stream[:, start:stop], mybir.AluOpType.min
+                room, values[:].indirect(listed(start, stop)), streamed(start, stop), mybir.AluOpType.min
             )
 
         def open_gates(start, stop):
@@ -39,37 +44,38 @@ def tile_lookup_vg_mintanh_out_kernel(tc, tab, y, offs, out):
                 opened[:, start:stop], gates[:].indirect(listed(start, stop)), mybir.ActivationFunctionType.Tanh
             )
 
-        def finish(start, stop, room):
-            nc.vector.tensor_tensor(room, clipped[:, start:stop], opened[:, start:stop], mybir.AluOpType.mult)
+        def finish(start, stop, minima, room):
+            nc.vector.tensor_tensor(room, minima, opened[:, start:stop], mybir.AluOpType.mult)
             nc.sync.dma_start(out[:, start:stop], room)
 
-        early = entries // 2 - NARROW
-        first = early + 2 * NARROW
-        second = first + 2 * NARROW
+        early = entries // 2
+        first = early + HALF
+        last = entries - WIDE
         nc.sync.dma_start(offsets[:], offs)
         nc.sync.dma_start(values[:], tab[0])
-        nc.scalar.dma_start(stream[:, :early], y[:, :early])
+        nc.scalar.dma_start(streamed(0, early), y[:, :early])
         nc.sync.dma_start(gates[:], tab[1])
-        for start, stop in ((early, first), (first, second), (second, entries)):
-            nc.sync.dma_start(stream[:, start:stop], y[:, start:stop])
+        for start, stop in ((early, first), (first, last), (last, entries)):
+            nc.sync.dma_start(streamed(start, stop), y[:, start:stop])
 
-        last = entries - WIDE
-        for start in range(0, last, WIDE // 2):
-            open_gates(start, start + WIDE // 2)
-        for start in range(last, entries, NARROW):
-            open_gates(start, start + NARROW)
+        taper = last + 3 * TINY
+        end = entries - NARROW
+        steps = list(range(0, last, HALF)) + [last, taper, end, entries - TINY, entries]
+        for start, stop in zip(steps, steps[1:]):
+            open_gates(start, stop)
 
-        used = first + NARROW
-        clip(0, early)
-        clip(early, first)
-        clip(first, used)
-        clip(used, second)
-        finish(0, WIDE, stream[:, used - WIDE : used])
-        clip(second, used + WIDE)
-        clip(used + WIDE, entries - NARROW)
-        finish(WIDE, 2 * WIDE, stream[:, used : used + WIDE])
-        finish(2 * WIDE, last, product[:, :WIDE])
-        clip(entries - NARROW, entries)
-        cuts = [last, entries - 2 * NARROW, entries - NARROW, entries]
-        for start, stop in zip(cuts, cuts[1:]):
-            finish(start, stop, product[:, start - 2 * WIDE : stop - 2 * WIDE])
+        clip(0, early, clipped[:, :early])
+        clip(early, first, clipped[:, early:first])
+        clip(first, first + TINY, clipped[:, first : first + TINY])
+        clip(first + TINY, last, clipped[:, first + TINY : last])
+        finish(0, WIDE, clipped[:, :WIDE], streamed(first + TINY - WIDE, first + TINY))
+        clip(entries - TINY, entries, clipped[:, entries - TINY :])
+        clip(taper, entries - TINY, clipped[:, taper : entries - TINY])
+        finish(WIDE, early, clipped[:, WIDE:early], stream[:, WIDE - TINY : 2 * WIDE - TINY])
+        finish(early, first, clipped[:, early:first], streamed(taper, entries - TINY))
+        late_minima = clipped[:, WIDE : WIDE + taper - last]
+        clip(last, taper, late_minima)
+        finish(first, last, clipped[:, first:last], opened[:, early:first])
+        finish(last, taper, late_minima, opened[:, : taper - last])
+        finish(taper, end, clipped[:, taper:end], opened[:, first : first + end - taper])
+        finish(end, entries, clipped[:, end:], opened[:, last : last + entries - end])

@@ -53,7 +53,7 @@ def tile_lookup_vg_mintanh_out_kernel(tc, tab, y, offs, out):
         last = entries - WIDE
         nc.sync.dma_start(offsets[:], offs)
         nc.sync.dma_start(values[:], tab[0])
-        nc.scalar.dma_start(streamed(0, early), y[:, :early])
+        nc.sync.dma_start(streamed(0, early), y[:, :early])
         nc.sync.dma_start(gates[:], tab[1])
         for start, stop in ((early, first), (first, last), (last, entries)):
             nc.sync.dma_start(streamed(start, stop), y[:, start:stop])
@@ -77,5 +77,5 @@ def tile_lookup_vg_mintanh_out_kernel(tc, tab, y, offs, out):
         clip(last, taper, late_minima)
         finish(first, last, clipped[:, first:last], opened[:, early:first])
         finish(last, taper, late_minima, opened[:, : taper - last])
-        finish(taper, end, clipped[:, taper:end], opened[:, first : first + end - taper])
-        finish(end, entries, clipped[:, end:], opened[:, last : last + entries - end])
+        finish(taper, end, clipped[:, taper:end], streamed(last, last + end - taper))
+        finish(end, entries, clipped[:, end:], opened[:, first : first + entries - end])

@@ -5,8 +5,8 @@ U16 = mybir.dt.uint16
 ENTRIES_PER_COLUMN = 16
 WIDE = 512
 HALF = WIDE // 2
-NARROW = WIDE // 4
 TINY = WIDE // 8
+SPARE = 2 * TINY
 
 
 def tile_lookup_vg_mintanh_out_kernel(tc, tab, y, offs, out):
@@ -23,7 +23,7 @@ def tile_lookup_vg_mintanh_out_kernel(tc, tab, y, offs, out):
         offsets = held.tile([rows, entries // ENTRIES_PER_COLUMN], U16, name="offsets")
         values = held.tile([rows, places], F32, name="values")
         gates = held.tile([rows, places], F32, name="gates")
-        stream = held.tile([rows, entries], F32, name="stream")
+        stream = held.tile([rows, SPARE + entries], F32, name="stream")
         clipped = held.tile([rows, entries], F32, name="clipped")
         opened = held.tile([rows, entries], F32, name="opened")
 
@@ -31,7 +31,7 @@ def tile_lookup_vg_mintanh_out_kernel(tc, tab, y, offs, out):
             return offsets[:, start // ENTRIES_PER_COLUMN : stop // ENTRIES_PER_COLUMN]
 
         def streamed(start, stop):
-            place = (start + WIDE) % entries
+            place = SPARE + (start + WIDE) % entries
             return stream[:, place : place + stop - start]
 
         def clip(start, stop, room):
@@ -48,34 +48,36 @@ def tile_lookup_vg_mintanh_out_kernel(tc, tab, y, offs, out):
             nc.vector.tensor_tensor(room, minima, opened[:, start:stop], mybir.AluOpType.mult)
             nc.sync.dma_start(out[:, start:stop], room)
 
-        early = entries // 2
-        first = early + HALF
+        half = entries // 2
+        early = half - TINY
+        short = early + 3 * TINY
         last = entries - WIDE
         nc.sync.dma_start(offsets[:], offs)
         nc.sync.dma_start(values[:], tab[0])
         nc.sync.dma_start(streamed(0, early), y[:, :early])
         nc.sync.dma_start(gates[:], tab[1])
-        for start, stop in ((early, first), (first, last), (last, entries)):
+        for start, stop in ((early, short), (short, last), (last, entries)):
             nc.sync.dma_start(streamed(start, stop), y[:, start:stop])
 
+        third = half + HALF
         taper = last + 3 * TINY
-        end = entries - NARROW
-        steps = list(range(0, last, HALF)) + [last, taper, end, entries - TINY, entries]
+        end = taper + 3 * TINY
+        steps = list(range(0, last, HALF)) + [last, taper, end, end + TINY, entries]
         for start, stop in zip(steps, steps[1:]):
             open_gates(start, stop)
 
         clip(0, early, clipped[:, :early])
-        clip(early, first, clipped[:, early:first])
-        clip(first, first + TINY, clipped[:, first : first + TINY])
-        clip(first + TINY, last, clipped[:, first + TINY : last])
-        finish(0, WIDE, clipped[:, :WIDE], streamed(first + TINY - WIDE, first + TINY))
+        clip(early, short, clipped[:, early:short])
+        clip(short, short + TINY, clipped[:, short : short + TINY])
+        clip(short + TINY, last, clipped[:, short + TINY : last])
+        finish(0, WIDE, clipped[:, :WIDE], streamed(short + TINY - WIDE, short + TINY))
         clip(entries - TINY, entries, clipped[:, entries - TINY :])
         clip(taper, entries - TINY, clipped[:, taper : entries - TINY])
-        finish(WIDE, early, clipped[:, WIDE:early], stream[:, WIDE - TINY : 2 * WIDE - TINY])
-        finish(early, first, clipped[:, early:first], streamed(taper, entries - TINY))
-        late_minima = clipped[:, WIDE : WIDE + taper - last]
-        clip(last, taper, late_minima)
-        finish(first, last, clipped[:, first:last], opened[:, early:first])
-        finish(last, taper, late_minima, opened[:, : taper - last])
-        finish(taper, end, clipped[:, taper:end], streamed(last, last + end - taper))
-        finish(end, entries, clipped[:, end:], opened[:, first : first + entries - end])
+        finish(WIDE, half, clipped[:, WIDE:half], stream[:, SPARE + WIDE - TINY : SPARE + 2 * WIDE - TINY])
+        finish(half, third, clipped[:, half:third], streamed(taper, entries - TINY))
+        last_minima = clipped[:, WIDE : WIDE + taper - last]
+        clip(last, taper, last_minima)
+        finish(third, last, clipped[:, third:last], opened[:, half:third])
+        finish(last, taper, last_minima, opened[:, : taper - last])
+        finish(taper, end, clipped[:, taper:end], stream[:, : end - taper])
+        finish(end, entries, clipped[:, end:], stream[:, end - taper : entries - taper])

@@ -3,10 +3,7 @@ import concourse.mybir as mybir
 F32 = mybir.dt.float32
 U16 = mybir.dt.uint16
 ENTRIES_PER_COLUMN = 16
-WIDE = 512
-HALF = WIDE // 2
-TINY = WIDE // 8
-SPARE = 2 * TINY
+STEP = 32
 
 
 def tile_lookup_vg_mintanh_out_kernel(tc, tab, y, offs, out):
@@ -23,20 +20,16 @@ def tile_lookup_vg_mintanh_out_kernel(tc, tab, y, offs, out):
         offsets = held.tile([rows, entries // ENTRIES_PER_COLUMN], U16, name="offsets")
         values = held.tile([rows, places], F32, name="values")
         gates = held.tile([rows, places], F32, name="gates")
-        stream = held.tile([rows, SPARE + entries], F32, name="stream")
+        stream = held.tile([rows, entries], F32, name="stream")
         clipped = held.tile([rows, entries], F32, name="clipped")
         opened = held.tile([rows, entries], F32, name="opened")
 
         def listed(start, stop):
             return offsets[:, start // ENTRIES_PER_COLUMN : stop // ENTRIES_PER_COLUMN]
 
-        def streamed(start, stop):
-            place = SPARE + (start + WIDE) % entries
-            return stream[:, place : place + stop - start]
-
         def clip(start, stop, room):
             nc.vector.tensor_tensor(
-                room, values[:].indirect(listed(start, stop)), streamed(start, stop), mybir.AluOpType.min
+                room, values[:].indirect(listed(start, stop)), stream[:, start:stop], mybir.AluOpType.min
             )
 
         def open_gates(start, stop):
@@ -48,36 +41,42 @@ def tile_lookup_vg_mintanh_out_kernel(tc, tab, y, offs, out):
             nc.vector.tensor_tensor(room, minima, opened[:, start:stop], mybir.AluOpType.mult)
             nc.sync.dma_start(out[:, start:stop], room)
 
-        half = entries // 2
-        early = half - TINY
-        short = early + 3 * TINY
-        last = entries - WIDE
+        front = 256
+        early = front + 1024
+        second = early + 128
+        third = second + 320
+        tail = entries - 128
+        cuts = [0, 480, 960, 1408, 1664, 1920, entries]
+
         nc.sync.dma_start(offsets[:], offs)
         nc.sync.dma_start(values[:], tab[0])
-        nc.sync.dma_start(streamed(0, early), y[:, :early])
+        nc.sync.dma_start(stream[:, front:early], y[:, front:early])
         nc.sync.dma_start(gates[:], tab[1])
-        for start, stop in ((early, short), (short, last), (last, entries)):
-            nc.sync.dma_start(streamed(start, stop), y[:, start:stop])
+        for start, stop in ((0, front), (early, second), (second, third), (third, entries)):
+            nc.sync.dma_start(stream[:, start:stop], y[:, start:stop])
 
-        third = half + HALF
-        taper = last + 3 * TINY
-        end = taper + 3 * TINY
-        steps = list(range(0, last, HALF)) + [last, taper, end, end + TINY, entries]
-        for start, stop in zip(steps, steps[1:]):
+        for start, stop in zip(cuts, cuts[1:]):
             open_gates(start, stop)
 
-        clip(0, early, clipped[:, :early])
-        clip(early, short, clipped[:, early:short])
-        clip(short, short + TINY, clipped[:, short : short + TINY])
-        clip(short + TINY, last, clipped[:, short + TINY : last])
-        finish(0, WIDE, clipped[:, :WIDE], streamed(short + TINY - WIDE, short + TINY))
-        clip(entries - TINY, entries, clipped[:, entries - TINY :])
-        clip(taper, entries - TINY, clipped[:, taper : entries - TINY])
-        finish(WIDE, half, clipped[:, WIDE:half], stream[:, SPARE + WIDE - TINY : SPARE + 2 * WIDE - TINY])
-        finish(half, third, clipped[:, half:third], streamed(taper, entries - TINY))
-        last_minima = clipped[:, WIDE : WIDE + taper - last]
-        clip(last, taper, last_minima)
-        finish(third, last, clipped[:, third:last], opened[:, half:third])
-        finish(last, taper, last_minima, opened[:, : taper - last])
-        finish(taper, end, clipped[:, taper:end], stream[:, : end - taper])
-        finish(end, entries, clipped[:, end:], stream[:, end - taper : entries - taper])
+        def width(k):
+            return cuts[k + 1] - cuts[k]
+
+        def product(k, room):
+            finish(cuts[k], cuts[k + 1], clipped[:, cuts[k] : cuts[k + 1]], room)
+
+        def over_tanh_of(k, columns):
+            return opened[:, cuts[k] : cuts[k] + columns]
+
+        clip(front, early, clipped[:, front:early])
+        clip(0, front, clipped[:, :front])
+        clip(early, second, clipped[:, early:second])
+        product(0, stream[:, front : front + width(0)])
+        clip(second, third, clipped[:, second:third])
+        product(1, over_tanh_of(0, width(1)))
+        clip(third, tail, clipped[:, third:tail])
+        product(2, over_tanh_of(1, width(2)))
+        product(3, stream[:, tail - width(3) : tail])
+        last_minima = over_tanh_of(2, entries - tail)
+        clip(tail, entries, last_minima)
+        product(4, over_tanh_of(3, width(4)))
+        finish(tail, entries, last_minima, stream[:, early - width(5) : early])

@@ -41,42 +41,35 @@ def tile_lookup_vg_mintanh_out_kernel(tc, tab, y, offs, out):
             nc.vector.tensor_tensor(room, minima, opened[:, start:stop], mybir.AluOpType.mult)
             nc.sync.dma_start(out[:, start:stop], room)
 
-        front = 256
-        early = front + 1024
-        second = early + 128
-        third = second + 320
-        tail = entries - 128
-        cuts = [0, 480, 960, 1408, 1664, 1920, entries]
+        early = 864
+        short = early + 192
+        mark = short + 2 * STEP
+        middle = short + 384
+        cuts = [0, 512, 1024, 1280, 1536, 1760, 1920, entries]
+        tail = cuts[5]
 
         nc.sync.dma_start(offsets[:], offs)
         nc.sync.dma_start(values[:], tab[0])
-        nc.sync.dma_start(stream[:, front:early], y[:, front:early])
+        nc.sync.dma_start(stream[:, :early], y[:, :early])
         nc.sync.dma_start(gates[:], tab[1])
-        for start, stop in ((0, front), (early, second), (second, third), (third, entries)):
+        for start, stop in ((early, short), (short, middle), (middle, entries)):
             nc.sync.dma_start(stream[:, start:stop], y[:, start:stop])
 
         for start, stop in zip(cuts, cuts[1:]):
             open_gates(start, stop)
 
-        def width(k):
-            return cuts[k + 1] - cuts[k]
+        def product(k, tile, place):
+            start, stop = cuts[k], cuts[k + 1]
+            finish(start, stop, clipped[:, start:stop], tile[:, place : place + stop - start])
 
-        def product(k, room):
-            finish(cuts[k], cuts[k + 1], clipped[:, cuts[k] : cuts[k + 1]], room)
-
-        def over_tanh_of(k, columns):
-            return opened[:, cuts[k] : cuts[k] + columns]
-
-        clip(front, early, clipped[:, front:early])
-        clip(0, front, clipped[:, :front])
-        clip(early, second, clipped[:, early:second])
-        product(0, stream[:, front : front + width(0)])
-        clip(second, third, clipped[:, second:third])
-        product(1, over_tanh_of(0, width(1)))
-        clip(third, tail, clipped[:, third:tail])
-        product(2, over_tanh_of(1, width(2)))
-        product(3, stream[:, tail - width(3) : tail])
-        last_minima = over_tanh_of(2, entries - tail)
-        clip(tail, entries, last_minima)
-        product(4, over_tanh_of(3, width(4)))
-        finish(tail, entries, last_minima, stream[:, early - width(5) : early])
+        for start, stop in ((0, early), (early, short), (short, mark), (mark, middle)):
+            clip(start, stop, clipped[:, start:stop])
+        product(0, stream, mark - cuts[1])
+        clip(middle, tail, clipped[:, middle:tail])
+        product(1, opened, 0)
+        product(2, clipped, 0)
+        clip(tail, entries, stream[:, middle : middle + entries - tail])
+        product(3, opened, cuts[1])
+        product(4, opened, cuts[2])
+        for start, stop in ((tail, cuts[6]), (cuts[6], entries)):
+            finish(start, stop, stream[:, middle + start - tail : middle + stop - tail], stream[:, start - tail : stop - tail])

@@ -4,6 +4,7 @@ F32 = mybir.dt.float32
 U16 = mybir.dt.uint16
 ENTRIES_PER_COLUMN = 16
 STEP = 32
+SPARE = 128
 
 
 def tile_lookup_vg_mintanh_out_kernel(tc, tab, y, offs, out):
@@ -22,7 +23,8 @@ def tile_lookup_vg_mintanh_out_kernel(tc, tab, y, offs, out):
         gates = held.tile([rows, places], F32, name="gates")
         stream = held.tile([rows, entries], F32, name="stream")
         clipped = held.tile([rows, entries], F32, name="clipped")
-        opened = held.tile([rows, entries], F32, name="opened")
+        tanh_tile = held.tile([rows, SPARE + entries], F32, name="tanh_tile")
+        opened = tanh_tile[:, SPARE:]
 
         def listed(start, stop):
             return offsets[:, start // ENTRIES_PER_COLUMN : stop // ENTRIES_PER_COLUMN]
@@ -41,12 +43,12 @@ def tile_lookup_vg_mintanh_out_kernel(tc, tab, y, offs, out):
             nc.vector.tensor_tensor(room, minima, opened[:, start:stop], mybir.AluOpType.mult)
             nc.sync.dma_start(out[:, start:stop], room)
 
-        early = 864
+        early = 960
         short = early + 192
         mark = short + 2 * STEP
-        middle = short + 384
-        cuts = [0, 512, 1024, 1280, 1536, 1760, 1920, entries]
-        tail = cuts[5]
+        middle = short + 320
+        cuts = [0, 384, 896, 1280, 1536, 1760, 1920, entries]
+        tail = cuts[6]
 
         nc.sync.dma_start(offsets[:], offs)
         nc.sync.dma_start(values[:], tab[0])
@@ -66,10 +68,10 @@ def tile_lookup_vg_mintanh_out_kernel(tc, tab, y, offs, out):
             clip(start, stop, clipped[:, start:stop])
         product(0, stream, mark - cuts[1])
         clip(middle, tail, clipped[:, middle:tail])
-        product(1, opened, 0)
+        product(1, tanh_tile, 0)
         product(2, clipped, 0)
-        clip(tail, entries, stream[:, middle : middle + entries - tail])
-        product(3, opened, cuts[1])
-        product(4, opened, cuts[2])
-        for start, stop in ((tail, cuts[6]), (cuts[6], entries)):
-            finish(start, stop, stream[:, middle + start - tail : middle + stop - tail], stream[:, start - tail : stop - tail])
+        last_minima = stream[:, middle : middle + entries - tail]
+        clip(tail, entries, last_minima)
+        for k in (3, 4, 5):
+            product(k, stream, cuts[k] - cuts[3])
+        finish(tail, entries, last_minima, stream[:, tail - cuts[3] : entries - cuts[3]])

@@ -39,9 +39,11 @@ def tile_lookup_vg_mintanh_out_kernel(tc, tab, y, offs, out):
                 opened[:, start:stop], gates[:].indirect(listed(start, stop)), mybir.ActivationFunctionType.Tanh
             )
 
-        def finish(start, stop, minima, room):
+        def finish(start, stop, minima, room, parts=1):
             nc.vector.tensor_tensor(room, minima, opened[:, start:stop], mybir.AluOpType.mult)
-            nc.sync.dma_start(out[:, start:stop], room)
+            part = (stop - start) // parts
+            for k in range(parts):
+                nc.sync.dma_start(out[:, start + k * part : start + (k + 1) * part], room[:, k * part : (k + 1) * part])
 
         early = 960
         short = early + 192
@@ -60,13 +62,13 @@ def tile_lookup_vg_mintanh_out_kernel(tc, tab, y, offs, out):
         for start, stop in zip(cuts, cuts[1:]):
             open_gates(start, stop)
 
-        def product(k, tile, place):
+        def product(k, tile, place, parts=1):
             start, stop = cuts[k], cuts[k + 1]
-            finish(start, stop, clipped[:, start:stop], tile[:, place : place + stop - start])
+            finish(start, stop, clipped[:, start:stop], tile[:, place : place + stop - start], parts)
 
         for start, stop in ((0, early), (early, short), (short, mark), (mark, middle)):
             clip(start, stop, clipped[:, start:stop])
-        product(0, stream, mark - cuts[1])
+        product(0, stream, mark - cuts[1], parts=3)
         clip(middle, tail, clipped[:, middle:tail])
         product(1, tanh_tile, 0)
         product(2, clipped, 0)

@@ -54,7 +54,7 @@ def tile_lookup_vg_mintanh_out_kernel(tc, tab, y, offs, out):
 
         nc.sync.dma_start(offsets[:], offs)
         nc.sync.dma_start(values[:], tab[0])
-        nc.sync.dma_start(stream[:, :early], y[:, :early])
+        nc.scalar.dma_start(stream[:, :early], y[:, :early])
         nc.sync.dma_start(gates[:], tab[1])
         for start, stop in ((early, short), (short, middle), (middle, entries)):
             nc.sync.dma_start(stream[:, start:stop], y[:, start:stop])

@@ -3,14 +3,23 @@ import concourse.mybir as mybir
 F32 = mybir.dt.float32
 U16 = mybir.dt.uint16
 ENTRIES_PER_COLUMN = 16
-STEP = 32
-SPARE = 128
+UNIT = 64
+
+
+def runs(start, units):
+    ends = [start + UNIT * sum(units[: k + 1]) for k in range(len(units))]
+    return list(zip([start] + ends, ends))
 
 
 def tile_lookup_vg_mintanh_out_kernel(tc, tab, y, offs, out):
     nc = tc.nc
     rows, places = tab.shape[1], tab.shape[2]
     entries = y.shape[1]
+
+    pieces = runs(0, (6, 8, 6, 4, 3, 3, 2))
+    early = 15 * UNIT
+    late = runs(early, (3, 5, 7, 2))
+    spare = (pieces[1][1] - pieces[1][0]) - pieces[0][1]
 
     with tc.tile_pool(name="held", bufs=1) as held:
         dummy = held.tile([rows, 1], F32, name="dummy")
@@ -23,15 +32,18 @@ def tile_lookup_vg_mintanh_out_kernel(tc, tab, y, offs, out):
         gates = held.tile([rows, places], F32, name="gates")
         stream = held.tile([rows, entries], F32, name="stream")
         clipped = held.tile([rows, entries], F32, name="clipped")
-        tanh_tile = held.tile([rows, SPARE + entries], F32, name="tanh_tile")
-        opened = tanh_tile[:, SPARE:]
+        spare_and_opened = held.tile([rows, spare + entries], F32, name="spare_and_opened")
+        opened = spare_and_opened[:, spare:]
 
         def listed(start, stop):
             return offsets[:, start // ENTRIES_PER_COLUMN : stop // ENTRIES_PER_COLUMN]
 
-        def clip(start, stop, room):
+        def clip(start, stop):
             nc.vector.tensor_tensor(
-                room, values[:].indirect(listed(start, stop)), stream[:, start:stop], mybir.AluOpType.min
+                clipped[:, start:stop],
+                values[:].indirect(listed(start, stop)),
+                stream[:, start:stop],
+                mybir.AluOpType.min,
             )
 
         def open_gates(start, stop):
@@ -39,41 +51,31 @@ def tile_lookup_vg_mintanh_out_kernel(tc, tab, y, offs, out):
                 opened[:, start:stop], gates[:].indirect(listed(start, stop)), mybir.ActivationFunctionType.Tanh
             )
 
-        def finish(start, stop, minima, room, parts=1):
-            nc.vector.tensor_tensor(room, minima, opened[:, start:stop], mybir.AluOpType.mult)
-            part = (stop - start) // parts
-            for k in range(parts):
-                nc.sync.dma_start(out[:, start + k * part : start + (k + 1) * part], room[:, k * part : (k + 1) * part])
-
-        early = 960
-        short = early + 192
-        mark = short + 2 * STEP
-        middle = short + 320
-        cuts = [0, 384, 896, 1280, 1536, 1760, 1920, entries]
-        tail = cuts[6]
+        def finish(piece, tile, place):
+            start, stop = piece
+            room = tile[:, place : place + stop - start]
+            nc.vector.tensor_tensor(room, clipped[:, start:stop], opened[:, start:stop], mybir.AluOpType.mult)
+            nc.sync.dma_start(out[:, start:stop], room)
 
         nc.sync.dma_start(offsets[:], offs)
         nc.sync.dma_start(values[:], tab[0])
         nc.scalar.dma_start(stream[:, :early], y[:, :early])
         nc.sync.dma_start(gates[:], tab[1])
-        for start, stop in ((early, short), (short, middle), (middle, entries)):
+        for start, stop in late:
             nc.sync.dma_start(stream[:, start:stop], y[:, start:stop])
 
-        for start, stop in zip(cuts, cuts[1:]):
+        for start, stop in pieces:
             open_gates(start, stop)
 
-        def product(k, tile, place, parts=1):
-            start, stop = cuts[k], cuts[k + 1]
-            finish(start, stop, clipped[:, start:stop], tile[:, place : place + stop - start], parts)
-
-        for start, stop in ((0, early), (early, short), (short, mark), (mark, middle)):
-            clip(start, stop, clipped[:, start:stop])
-        product(0, stream, mark - cuts[1], parts=3)
-        clip(middle, tail, clipped[:, middle:tail])
-        product(1, tanh_tile, 0)
-        product(2, clipped, 0)
-        last_minima = stream[:, middle : middle + entries - tail]
-        clip(tail, entries, last_minima)
-        for k in (3, 4, 5):
-            product(k, stream, cuts[k] - cuts[3])
-        finish(tail, entries, last_minima, stream[:, tail - cuts[3] : entries - cuts[3]])
+        marked = late[1][0] + UNIT
+        clip(0, early)
+        clip(*late[0])
+        clip(late[1][0], marked)
+        clip(marked, late[1][1])
+        finish(pieces[0], stream, marked - pieces[0][1])
+        clip(*late[2])
+        finish(pieces[1], spare_and_opened, 0)
+        finish(pieces[2], clipped, 0)
+        clip(*late[3])
+        for piece in pieces[3:]:
+            finish(piece, stream, piece[0] - pieces[3][0])

@@ -3,7 +3,8 @@ import concourse.mybir as mybir
 F32 = mybir.dt.float32
 U16 = mybir.dt.uint16
 ENTRIES_PER_COLUMN = 16
-UNIT = 64
+UNIT = 32
+MARK = 2 * UNIT
 
 
 def runs(start, units):
@@ -16,9 +17,9 @@ def tile_lookup_vg_mintanh_out_kernel(tc, tab, y, offs, out):
     rows, places = tab.shape[1], tab.shape[2]
     entries = y.shape[1]
 
-    pieces = runs(0, (6, 8, 6, 4, 3, 3, 2))
-    early = 15 * UNIT
-    late = runs(early, (3, 5, 7, 2))
+    pieces = runs(0, (12, 16, 12, 8, 7, 5, 4))
+    early = 29 * UNIT
+    late = runs(early, (6, 10, 15, 4))
     spare = (pieces[1][1] - pieces[1][0]) - pieces[0][1]
 
     with tc.tile_pool(name="held", bufs=1) as held:
@@ -67,7 +68,7 @@ def tile_lookup_vg_mintanh_out_kernel(tc, tab, y, offs, out):
         for start, stop in pieces:
             open_gates(start, stop)
 
-        marked = late[1][0] + UNIT
+        marked = late[1][0] + MARK
         clip(0, early)
         clip(*late[0])
         clip(late[1][0], marked)

@@ -18,8 +18,8 @@ def tile_lookup_vg_mintanh_out_kernel(tc, tab, y, offs, out):
     entries = y.shape[1]
 
     pieces = runs(0, (12, 16, 12, 8, 7, 5, 4))
-    early = 29 * UNIT
-    late = runs(early, (6, 10, 15, 4))
+    early = 30 * UNIT
+    late = runs(early, (6, 10, 14, 4))
     spare = (pieces[1][1] - pieces[1][0]) - pieces[0][1]
 
     with tc.tile_pool(name="held", bufs=1) as held:

@@ -4,7 +4,6 @@ F32 = mybir.dt.float32
 U16 = mybir.dt.uint16
 ENTRIES_PER_COLUMN = 16
 UNIT = 32
-MARK = 2 * UNIT
 
 
 def runs(start, units):
@@ -18,8 +17,10 @@ def tile_lookup_vg_mintanh_out_kernel(tc, tab, y, offs, out):
     entries = y.shape[1]
 
     pieces = runs(0, (12, 16, 12, 8, 7, 5, 4))
-    early = 30 * UNIT
-    late = runs(early, (6, 10, 14, 4))
+    early = 29 * UNIT
+    ahead = runs(early, (6, 2, 6))
+    between = runs(ahead[-1][1], (8, 5, 4, 4))
+    loads = [ahead[0], (ahead[1][0], ahead[2][1]), (between[0][0], between[-2][1]), between[-1]]
     spare = (pieces[1][1] - pieces[1][0]) - pieces[0][1]
 
     with tc.tile_pool(name="held", bufs=1) as held:
@@ -35,6 +36,7 @@ def tile_lookup_vg_mintanh_out_kernel(tc, tab, y, offs, out):
         clipped = held.tile([rows, entries], F32, name="clipped")
         spare_and_opened = held.tile([rows, spare + entries], F32, name="spare_and_opened")
         opened = spare_and_opened[:, spare:]
+        products = held.tile([rows, entries], F32, name="products")
 
         def listed(start, stop):
             return offsets[:, start // ENTRIES_PER_COLUMN : stop // ENTRIES_PER_COLUMN]
@@ -47,11 +49,6 @@ def tile_lookup_vg_mintanh_out_kernel(tc, tab, y, offs, out):
                 mybir.AluOpType.min,
             )
 
-        def open_gates(start, stop):
-            nc.scalar.activation(
-                opened[:, start:stop], gates[:].indirect(listed(start, stop)), mybir.ActivationFunctionType.Tanh
-            )
-
         def finish(piece, tile, place):
             start, stop = piece
             room = tile[:, place : place + stop - start]
@@ -62,21 +59,20 @@ def tile_lookup_vg_mintanh_out_kernel(tc, tab, y, offs, out):
         nc.sync.dma_start(values[:], tab[0])
         nc.scalar.dma_start(stream[:, :early], y[:, :early])
         nc.sync.dma_start(gates[:], tab[1])
-        for start, stop in late:
+        for start, stop in loads:
             nc.sync.dma_start(stream[:, start:stop], y[:, start:stop])
 
         for start, stop in pieces:
-            open_gates(start, stop)
+            nc.scalar.activation(
+                opened[:, start:stop], gates[:].indirect(listed(start, stop)), mybir.ActivationFunctionType.Tanh
+            )
 
-        marked = late[1][0] + MARK
         clip(0, early)
-        clip(*late[0])
-        clip(late[1][0], marked)
-        clip(marked, late[1][1])
-        finish(pieces[0], stream, marked - pieces[0][1])
-        clip(*late[2])
-        finish(pieces[1], spare_and_opened, 0)
-        finish(pieces[2], clipped, 0)
-        clip(*late[3])
-        for piece in pieces[3:]:
-            finish(piece, stream, piece[0] - pieces[3][0])
+        for run in ahead:
+            clip(*run)
+        rooms = [(stream, ahead[1][1] - pieces[0][1]), (spare_and_opened, 0)]
+        rooms += [(products, start) for start, stop in pieces[2:]]
+        for k, piece in enumerate(pieces):
+            finish(piece, *rooms[k])
+            if k < len(between):
+                clip(*between[k])

@@ -19,8 +19,9 @@ def tile_lookup_vg_mintanh_out_kernel(tc, tab, y, offs, out):
     pieces = runs(0, (12, 16, 12, 8, 7, 5, 4))
     early = 29 * UNIT
     ahead = runs(early, (6, 2, 6))
-    between = runs(ahead[-1][1], (8, 5, 4, 4))
-    loads = [ahead[0], (ahead[1][0], ahead[2][1]), (between[0][0], between[-2][1]), between[-1]]
+    between = runs(ahead[-1][1], (8, 7, 4, 2))
+    loads = [ahead[0], (ahead[1][0], ahead[2][1]), (between[0][0], between[1][1])]
+    last = between[2][0]
     spare = (pieces[1][1] - pieces[1][0]) - pieces[0][1]
 
     with tc.tile_pool(name="held", bufs=1) as held:
@@ -32,8 +33,9 @@ def tile_lookup_vg_mintanh_out_kernel(tc, tab, y, offs, out):
         offsets = held.tile([rows, entries // ENTRIES_PER_COLUMN], U16, name="offsets")
         values = held.tile([rows, places], F32, name="values")
         gates = held.tile([rows, places], F32, name="gates")
-        stream = held.tile([rows, entries], F32, name="stream")
-        clipped = held.tile([rows, entries], F32, name="clipped")
+        stream = held.tile([rows, last], F32, name="stream")
+        clipped = held.tile([rows, between[-1][0] + entries - last], F32, name="clipped")
+        end_of_y = clipped[:, between[-1][0] :]
         spare_and_opened = held.tile([rows, spare + entries], F32, name="spare_and_opened")
         opened = spare_and_opened[:, spare:]
         products = held.tile([rows, entries], F32, name="products")
@@ -45,7 +47,7 @@ def tile_lookup_vg_mintanh_out_kernel(tc, tab, y, offs, out):
             nc.vector.tensor_tensor(
                 clipped[:, start:stop],
                 values[:].indirect(listed(start, stop)),
-                stream[:, start:stop],
+                stream[:, start:stop] if start < last else end_of_y[:, start - last : stop - last],
                 mybir.AluOpType.min,
             )
 
@@ -61,6 +63,7 @@ def tile_lookup_vg_mintanh_out_kernel(tc, tab, y, offs, out):
         nc.sync.dma_start(gates[:], tab[1])
         for start, stop in loads:
             nc.sync.dma_start(stream[:, start:stop], y[:, start:stop])
+        nc.sync.dma_start(end_of_y, y[:, last:])
 
         for start, stop in pieces:
             nc.scalar.activation(
@@ -72,7 +75,8 @@ def tile_lookup_vg_mintanh_out_kernel(tc, tab, y, offs, out):
             clip(*run)
         rooms = [(stream, ahead[1][1] - pieces[0][1]), (spare_and_opened, 0)]
         rooms += [(products, start) for start, stop in pieces[2:]]
+        followers = {0: between[0], 1: between[1], 3: between[2], 4: between[3]}
         for k, piece in enumerate(pieces):
             finish(piece, *rooms[k])
-            if k < len(between):
-                clip(*between[k])
+            if k in followers:
+                clip(*followers[k])

@@ -17,11 +17,11 @@ def tile_lookup_vg_mintanh_out_kernel(tc, tab, y, offs, out):
     entries = y.shape[1]
 
     pieces = runs(0, (12, 16, 12, 8, 7, 5, 4))
-    early = 29 * UNIT
+    early = 28 * UNIT
     ahead = runs(early, (6, 2, 6))
-    between = runs(ahead[-1][1], (8, 7, 4, 2))
-    loads = [ahead[0], (ahead[1][0], ahead[2][1]), (between[0][0], between[1][1])]
-    last = between[2][0]
+    between = runs(ahead[-1][1], (8, 5, 3, 4, 2))
+    loads = [ahead[0], (ahead[1][0], ahead[2][1]), (between[0][0], between[2][1])]
+    last = between[3][0]
     spare = (pieces[1][1] - pieces[1][0]) - pieces[0][1]
 
     with tc.tile_pool(name="held", bufs=1) as held:
@@ -75,8 +75,7 @@ def tile_lookup_vg_mintanh_out_kernel(tc, tab, y, offs, out):
             clip(*run)
         rooms = [(stream, ahead[1][1] - pieces[0][1]), (spare_and_opened, 0)]
         rooms += [(products, start) for start, stop in pieces[2:]]
-        followers = {0: between[0], 1: between[1], 3: between[2], 4: between[3]}
         for k, piece in enumerate(pieces):
             finish(piece, *rooms[k])
-            if k in followers:
-                clip(*followers[k])
+            if k < len(between):
+                clip(*between[k])

@@ -16,45 +16,42 @@ def tile_lookup_vg_mintanh_out_kernel(tc, tab, y, offs, out):
     rows, places = tab.shape[1], tab.shape[2]
     entries = y.shape[1]
 
-    pieces = runs(0, (12, 16, 12, 8, 7, 5, 4))
-    early = 28 * UNIT
-    ahead = runs(early, (6, 2, 6))
-    between = runs(ahead[-1][1], (8, 5, 3, 4, 2))
-    loads = [ahead[0], (ahead[1][0], ahead[2][1]), (between[0][0], between[2][1])]
-    last = between[3][0]
-    spare = (pieces[1][1] - pieces[1][0]) - pieces[0][1]
+    low, high, *pieces = runs(0, (14, 14, 12, 8, 7, 5, 4))
+    early = high[1]
+    short, long, first, second, *between = runs(early, (2, 12, 6, 8, 2, 4, 2))
+    ahead = [first, second, short, long]
+    loads = [first, second, (short[0], long[1]), (between[0][0], entries)]
+    tanh, mult = mybir.ActivationFunctionType.Tanh, mybir.AluOpType.mult
 
     with tc.tile_pool(name="held", bufs=1) as held:
         dummy = held.tile([rows, 1], F32, name="dummy")
         dummy_tanh = held.tile([rows, 1], F32, name="dummy_tanh")
         nc.vector.memset(dummy[:], 0.0)
-        nc.scalar.activation(dummy_tanh[:], dummy[:], mybir.ActivationFunctionType.Tanh)
+        nc.scalar.activation(dummy_tanh[:], dummy[:], tanh)
 
         offsets = held.tile([rows, entries // ENTRIES_PER_COLUMN], U16, name="offsets")
         values = held.tile([rows, places], F32, name="values")
         gates = held.tile([rows, places], F32, name="gates")
-        stream = held.tile([rows, last], F32, name="stream")
-        clipped = held.tile([rows, between[-1][0] + entries - last], F32, name="clipped")
-        end_of_y = clipped[:, between[-1][0] :]
-        spare_and_opened = held.tile([rows, spare + entries], F32, name="spare_and_opened")
-        opened = spare_and_opened[:, spare:]
-        products = held.tile([rows, entries], F32, name="products")
+        stream = held.tile([rows, entries], F32, name="stream")
+        clipped = held.tile([rows, between[0][0] + early], F32, name="clipped")
+        first_opened = clipped[:, between[0][0] :]
+        opened = held.tile([rows, entries - early], F32, name="opened")
+        products = held.tile([rows, entries - early], F32, name="products")
 
         def listed(start, stop):
             return offsets[:, start // ENTRIES_PER_COLUMN : stop // ENTRIES_PER_COLUMN]
 
+        def tanh_values(start, stop):
+            return first_opened[:, start:stop] if start < early else opened[:, start - early : stop - early]
+
         def clip(start, stop):
             nc.vector.tensor_tensor(
-                clipped[:, start:stop],
-                values[:].indirect(listed(start, stop)),
-                stream[:, start:stop] if start < last else end_of_y[:, start - last : stop - last],
-                mybir.AluOpType.min,
+                clipped[:, start:stop], values[:].indirect(listed(start, stop)), stream[:, start:stop], mybir.AluOpType.min
             )
 
-        def finish(piece, tile, place):
-            start, stop = piece
+        def finish(start, stop, tile, place):
             room = tile[:, place : place + stop - start]
-            nc.vector.tensor_tensor(room, clipped[:, start:stop], opened[:, start:stop], mybir.AluOpType.mult)
+            nc.vector.tensor_tensor(room, clipped[:, start:stop], tanh_values(start, stop), mult)
             nc.sync.dma_start(out[:, start:stop], room)
 
         nc.sync.dma_start(offsets[:], offs)
@@ -63,19 +60,16 @@ def tile_lookup_vg_mintanh_out_kernel(tc, tab, y, offs, out):
         nc.sync.dma_start(gates[:], tab[1])
         for start, stop in loads:
             nc.sync.dma_start(stream[:, start:stop], y[:, start:stop])
-        nc.sync.dma_start(end_of_y, y[:, last:])
 
-        for start, stop in pieces:
-            nc.scalar.activation(
-                opened[:, start:stop], gates[:].indirect(listed(start, stop)), mybir.ActivationFunctionType.Tanh
-            )
+        for start, stop in [(0, early)] + pieces:
+            nc.scalar.activation(tanh_values(start, stop), gates[:].indirect(listed(start, stop)), tanh)
 
         clip(0, early)
         for run in ahead:
             clip(*run)
-        rooms = [(stream, ahead[1][1] - pieces[0][1]), (spare_and_opened, 0)]
-        rooms += [(products, start) for start, stop in pieces[2:]]
+        finish(*high, stream, short[1] - (high[1] - high[0]))
+        finish(*low, stream, long[0])
         for k, piece in enumerate(pieces):
-            finish(piece, *rooms[k])
+            finish(*piece, products, piece[0] - early)
             if k < len(between):
                 clip(*between[k])

@@ -16,9 +16,10 @@ def tile_lookup_vg_mintanh_out_kernel(tc, tab, y, offs, out):
     rows, places = tab.shape[1], tab.shape[2]
     entries = y.shape[1]
 
-    low, high, *pieces = runs(0, (14, 14, 12, 8, 7, 5, 4))
-    early = high[1]
-    short, long, first, second, *between = runs(early, (2, 12, 6, 8, 2, 4, 2))
+    low, high, *pieces = runs(0, (13, 13, 11, 11, 7, 5, 4))
+    shared = high[1]
+    early = 28 * UNIT
+    short, long, first, second, *between = runs(early, (2, 10, 6, 8, 5, 3, 2))
     ahead = [first, second, short, long]
     loads = [first, second, (short[0], long[1]), (between[0][0], entries)]
     tanh, mult = mybir.ActivationFunctionType.Tanh, mybir.AluOpType.mult
@@ -33,16 +34,16 @@ def tile_lookup_vg_mintanh_out_kernel(tc, tab, y, offs, out):
         values = held.tile([rows, places], F32, name="values")
         gates = held.tile([rows, places], F32, name="gates")
         stream = held.tile([rows, entries], F32, name="stream")
-        clipped = held.tile([rows, between[0][0] + early], F32, name="clipped")
+        clipped = held.tile([rows, between[0][0] + shared], F32, name="clipped")
         first_opened = clipped[:, between[0][0] :]
-        opened = held.tile([rows, entries - early], F32, name="opened")
-        products = held.tile([rows, entries - early], F32, name="products")
+        opened = held.tile([rows, entries - shared], F32, name="opened")
+        products = held.tile([rows, entries - shared], F32, name="products")
 
         def listed(start, stop):
             return offsets[:, start // ENTRIES_PER_COLUMN : stop // ENTRIES_PER_COLUMN]
 
         def tanh_values(start, stop):
-            return first_opened[:, start:stop] if start < early else opened[:, start - early : stop - early]
+            return first_opened[:, start:stop] if start < shared else opened[:, start - shared : stop - shared]
 
         def clip(start, stop):
             nc.vector.tensor_tensor(
@@ -61,7 +62,7 @@ def tile_lookup_vg_mintanh_out_kernel(tc, tab, y, offs, out):
         for start, stop in loads:
             nc.sync.dma_start(stream[:, start:stop], y[:, start:stop])
 
-        for start, stop in [(0, early)] + pieces:
+        for start, stop in [(0, shared)] + pieces:
             nc.scalar.activation(tanh_values(start, stop), gates[:].indirect(listed(start, stop)), tanh)
 
         clip(0, early)
@@ -70,6 +71,6 @@ def tile_lookup_vg_mintanh_out_kernel(tc, tab, y, offs, out):
         finish(*high, stream, short[1] - (high[1] - high[0]))
         finish(*low, stream, long[0])
         for k, piece in enumerate(pieces):
-            finish(*piece, products, piece[0] - early)
+            finish(*piece, products, piece[0] - shared)
             if k < len(between):
                 clip(*between[k])

@@ -16,10 +16,10 @@ def tile_lookup_vg_mintanh_out_kernel(tc, tab, y, offs, out):
     rows, places = tab.shape[1], tab.shape[2]
     entries = y.shape[1]
 
-    low, high, *pieces = runs(0, (13, 13, 11, 11, 7, 5, 4))
+    low, high, *pieces = runs(0, (12, 13, 11, 11, 8, 5, 4))
     shared = high[1]
     early = 28 * UNIT
-    short, long, first, second, *between = runs(early, (2, 10, 6, 8, 5, 3, 2))
+    short, long, first, second, *between = runs(early, (2, 9, 6, 8, 6, 3, 2))
     ahead = [first, second, short, long]
     loads = [first, second, (short[0], long[1]), (between[0][0], entries)]
     tanh, mult = mybir.ActivationFunctionType.Tanh, mybir.AluOpType.mult

@@ -4,6 +4,8 @@ F32 = mybir.dt.float32
 U16 = mybir.dt.uint16
 ENTRIES_PER_COLUMN = 16
 UNIT = 32
+BURST = 256
+BURST_COLUMNS = BURST // 4
 
 
 def runs(start, units):
@@ -30,14 +32,15 @@ def tile_lookup_vg_mintanh_out_kernel(tc, tab, y, offs, out):
         nc.vector.memset(dummy[:], 0.0)
         nc.scalar.activation(dummy_tanh[:], dummy[:], tanh)
 
-        offsets = held.tile([rows, entries // ENTRIES_PER_COLUMN], U16, name="offsets")
-        values = held.tile([rows, places], F32, name="values")
-        gates = held.tile([rows, places], F32, name="gates")
-        stream = held.tile([rows, entries], F32, name="stream")
+        offsets = held.tile([rows, entries // ENTRIES_PER_COLUMN], U16, name="offsets", align_bytes=BURST)
+        values = held.tile([rows, places], F32, name="values", align_bytes=BURST)
+        gates = held.tile([rows, places], F32, name="gates", align_bytes=BURST)
+        stream = held.tile([rows, entries], F32, name="stream", align_bytes=BURST)
         clipped = held.tile([rows, between[0][0] + shared], F32, name="clipped")
         first_opened = clipped[:, between[0][0] :]
         opened = held.tile([rows, entries - shared], F32, name="opened")
-        products = held.tile([rows, entries - shared], F32, name="products")
+        rooms = [BURST_COLUMNS * sum(-((a - b) // BURST_COLUMNS) for a, b in pieces[:k]) for k in range(len(pieces) + 1)]
+        products = held.tile([rows, rooms[-1]], F32, name="products", align_bytes=BURST)
 
         def listed(start, stop):
             return offsets[:, start // ENTRIES_PER_COLUMN : stop // ENTRIES_PER_COLUMN]
@@ -68,9 +71,9 @@ def tile_lookup_vg_mintanh_out_kernel(tc, tab, y, offs, out):
         clip(0, early)
         for run in ahead:
             clip(*run)
-        finish(*high, stream, short[1] - (high[1] - high[0]))
+        finish(*high, stream, (short[1] - (high[1] - high[0])) // BURST_COLUMNS * BURST_COLUMNS)
         finish(*low, stream, long[0])
         for k, piece in enumerate(pieces):
-            finish(*piece, products, piece[0] - shared)
+            finish(*piece, products, rooms[k])
             if k < len(between):
                 clip(*between[k])

@@ -18,10 +18,10 @@ def tile_lookup_vg_mintanh_out_kernel(tc, tab, y, offs, out):
     rows, places = tab.shape[1], tab.shape[2]
     entries = y.shape[1]
 
-    low, high, *pieces = runs(0, (12, 13, 11, 11, 8, 5, 4))
+    low, high, *pieces = runs(0, (12, 14, 12, 10, 7, 5, 4))
     shared = high[1]
-    early = 28 * UNIT
-    short, long, first, second, *between = runs(early, (2, 9, 6, 8, 6, 3, 2))
+    early = 30 * UNIT
+    short, long, first, second, *between = runs(early, (2, 10, 6, 8, 4, 2, 2))
     ahead = [first, second, short, long]
     loads = [first, second, (short[0], long[1]), (between[0][0], entries)]
     tanh, mult = mybir.ActivationFunctionType.Tanh, mybir.AluOpType.mult

@@ -21,7 +21,7 @@ def tile_lookup_vg_mintanh_out_kernel(tc, tab, y, offs, out):
     low, high, *pieces = runs(0, (12, 14, 12, 10, 7, 5, 4))
     shared = high[1]
     early = 30 * UNIT
-    short, long, first, second, *between = runs(early, (2, 10, 6, 8, 4, 2, 2))
+    first, short, long, second, *between = runs(early, (6, 2, 10, 8, 4, 2, 2))
     ahead = [first, second, short, long]
     loads = [first, second, (short[0], long[1]), (between[0][0], entries)]
     tanh, mult = mybir.ActivationFunctionType.Tanh, mybir.AluOpType.mult

@@ -54,9 +54,9 @@ def tile_lookup_vg_mintanh_out_kernel(tc, tab, y, offs, out):
             )
 
         def finish(start, stop, tile, place):
-            room = tile[:, place : place + stop - start]
-            nc.vector.tensor_tensor(room, clipped[:, start:stop], tanh_values(start, stop), mult)
-            nc.sync.dma_start(out[:, start:stop], room)
+            for a, b in between[-2:] if stop == entries else [(start, stop)]:
+                nc.vector.tensor_tensor(tile[:, place + a - start : place + b - start], clipped[:, a:b], tanh_values(a, b), mult)
+            nc.sync.dma_start(out[:, start:stop], tile[:, place : place + stop - start])
 
         nc.sync.dma_start(offsets[:], offs)
         nc.sync.dma_start(values[:], tab[0])

@@ -20,8 +20,8 @@ def tile_lookup_vg_mintanh_out_kernel(tc, tab, y, offs, out):
 
     low, high, *pieces = runs(0, (12, 14, 12, 10, 7, 5, 4))
     shared = high[1]
-    early = 30 * UNIT
-    first, short, long, second, *between = runs(early, (6, 2, 10, 8, 4, 2, 2))
+    early = 28 * UNIT
+    first, short, long, second, *between = runs(early, (6, 2, 10, 8, 6, 2, 2))
     ahead = [first, second, short, long]
     loads = [first, second, (short[0], long[1]), (between[0][0], entries)]
     tanh, mult = mybir.ActivationFunctionType.Tanh, mybir.AluOpType.mult

import concourse.mybir as mybir

F32 = mybir.dt.float32
U16 = mybir.dt.uint16
ENTRIES_PER_COLUMN = 16
UNIT = 32
BURST = 256
BURST_COLUMNS = BURST // 4


def runs(start, units):
    ends = [start + UNIT * sum(units[: k + 1]) for k in range(len(units))]
    return list(zip([start] + ends, ends))


def tile_lookup_vg_mintanh_out_kernel(tc, tab, y, offs, out):
    nc = tc.nc
    rows, places = tab.shape[1], tab.shape[2]
    entries = y.shape[1]

    low, high, *pieces = runs(0, (12, 14, 12, 10, 7, 5, 4))
    shared = high[1]
    early = 28 * UNIT
    first, short, long, second, *between = runs(early, (6, 2, 10, 8, 6, 2, 2))
    ahead = [first, second, short, long]
    loads = [first, second, (short[0], long[1]), (between[0][0], entries)]
    tanh, mult = mybir.ActivationFunctionType.Tanh, mybir.AluOpType.mult

    with tc.tile_pool(name="held", bufs=1) as held:
        dummy = held.tile([rows, 1], F32, name="dummy")
        dummy_tanh = held.tile([rows, 1], F32, name="dummy_tanh")
        nc.vector.memset(dummy[:], 0.0)
        nc.scalar.activation(dummy_tanh[:], dummy[:], tanh)

        offsets = held.tile([rows, entries // ENTRIES_PER_COLUMN], U16, name="offsets", align_bytes=BURST)
        values = held.tile([rows, places], F32, name="values", align_bytes=BURST)
        gates = held.tile([rows, places], F32, name="gates", align_bytes=BURST)
        stream = held.tile([rows, entries], F32, name="stream", align_bytes=BURST)
        clipped = held.tile([rows, between[0][0] + shared], F32, name="clipped")
        first_opened = clipped[:, between[0][0] :]
        opened = held.tile([rows, entries - shared], F32, name="opened")
        rooms = [BURST_COLUMNS * sum(-((a - b) // BURST_COLUMNS) for a, b in pieces[:k]) for k in range(len(pieces) + 1)]
        products = held.tile([rows, rooms[-1]], F32, name="products", align_bytes=BURST)

        def listed(start, stop):
            return offsets[:, start // ENTRIES_PER_COLUMN : stop // ENTRIES_PER_COLUMN]

        def tanh_values(start, stop):
            return first_opened[:, start:stop] if start < shared else opened[:, start - shared : stop - shared]

        def clip(start, stop):
            nc.vector.tensor_tensor(
                clipped[:, start:stop], values[:].indirect(listed(start, stop)), stream[:, start:stop], mybir.AluOpType.min
            )

        def finish(start, stop, tile, place):
            for a, b in between[-2:] if stop == entries else [(start, stop)]:
                nc.vector.tensor_tensor(tile[:, place + a - start : place + b - start], clipped[:, a:b], tanh_values(a, b), mult)
            nc.sync.dma_start(out[:, start:stop], tile[:, place : place + stop - start])

        nc.sync.dma_start(offsets[:], offs)
        nc.sync.dma_start(values[:], tab[0])
        nc.scalar.dma_start(stream[:, :early], y[:, :early])
        nc.sync.dma_start(gates[:], tab[1])
        for start, stop in loads:
            nc.sync.dma_start(stream[:, start:stop], y[:, start:stop])

        for start, stop in [(0, shared)] + pieces:
            nc.scalar.activation(tanh_values(start, stop), gates[:].indirect(listed(start, stop)), tanh)

        clip(0, early)
        for run in ahead:
            clip(*run)
        finish(*high, stream, (short[1] - (high[1] - high[0])) // BURST_COLUMNS * BURST_COLUMNS)
        finish(*low, stream, long[0])
        for k, piece in enumerate(pieces):
            finish(*piece, products, rooms[k])
            if k < len(between):
                clip(*between[k])
